import numpy as np
import ml_dtypes


def mxq(x, axis, fmt="e4m3"):
    dtype, down = {"e4m3": (ml_dtypes.float8_e4m3fn, 7), "e5m2": (ml_dtypes.float8_e5m2, 14)}[fmt]
    v = np.moveaxis(np.asarray(x, np.float32).astype(ml_dtypes.bfloat16).astype(np.float64), axis, -1)
    blocks = v.reshape(v.shape[:-1] + (-1, 32))
    amax = np.abs(blocks).max(-1, keepdims=True)
    byte = np.maximum(np.where(amax > 0, np.frexp(amax)[1] - 1 + 127, 0) - down, 1)
    scale = np.exp2(byte - 127.0)
    codes = (blocks / scale).astype(np.float32).astype(dtype).astype(np.float64)
    return np.moveaxis((codes * scale).reshape(v.shape), -1, axis)


WIDE = False


def mx_kscale(k):
    if not WIDE:
        return np.ones(k)
    levels = np.array([24, -24, 12, -12, 0])
    if k % 512:
        return np.exp2(np.random.permutation(np.resize(levels, k // 32))).repeat(32)
    a = np.empty((k // 512, 16))
    for p in range(k // 512):
        a[p, :8] = np.random.permutation(np.resize(levels, 8))
        for g in range(8):
            far = levels[np.abs(levels - a[p, g]) >= 10]
            a[p, g + 8] = far[np.random.randint(len(far))]
    return np.exp2(a.ravel()).repeat(32)


def f64(x):
    return np.asarray(x).astype(np.float64)


def striped(idx):
    return np.tile(idx.reshape(-1, 16).T, (8, 1)).astype(np.uint16)


def unstriped(offs):
    return offs[:16].T.reshape(-1).astype(np.int64)


E2M1 = np.array([0.0, 0.5, 1.0, 1.5, 2.0, 3.0, 4.0, 6.0, -0.0, -0.5, -1.0, -1.5, -2.0, -3.0, -4.0, -6.0])


def pack_weight(w, fmt):
    k, n = w.shape
    w = f64(np.asarray(w, np.float32).astype(ml_dtypes.bfloat16)).reshape(k // 32, 32, n)
    amax = np.abs(w).max(1)
    if fmt == "e4m3":
        byte = np.frexp(amax)[1] - 1 + 127 - 7
    else:
        mant, ex = np.frexp(amax / 6.0)
        byte = np.where(mant > 0.5, ex, ex - 1) + 127
    byte = np.clip(np.where(amax > 0, byte, 1), 1, 254)
    scaled = (w * np.exp2(127.0 - byte)[:, None, :]).reshape(k, n).astype(np.float32)
    by_word = np.ascontiguousarray(scaled.reshape(k // 512, 128, 4, n).transpose(0, 1, 3, 2))
    if fmt == "e4m3":
        words = by_word.astype(ml_dtypes.float8_e4m3fn).view(np.uint8)
    else:
        c = by_word.astype(ml_dtypes.float4_e2m1fn).view(np.uint8) & 0xF
        words = (c[..., 0::2] | (c[..., 1::2] << 4)).reshape(k // 512, 128, 2 * n)
    return np.ascontiguousarray(words), np.ascontiguousarray(byte.astype(np.uint8).reshape(k // 512, 16, n))


def unpack_weight(words, scales, fmt):
    g, _, n = scales.shape
    words = np.ascontiguousarray(words).reshape(g, 128, n, -1)
    if fmt == "e4m3":
        vals = words.view(ml_dtypes.float8_e4m3fn).astype(np.float64)
    else:
        nib = np.empty((g, 128, n, 4), np.uint8)
        nib[..., 0::2] = words & 0xF
        nib[..., 1::2] = words >> 4
        vals = E2M1[nib]
    vals = vals * np.repeat(np.exp2(scales.astype(np.float64) - 127.0), 8, axis=1)[..., None]
    return vals.transpose(0, 1, 3, 2).reshape(g * 512, n)


def split(x):
    m, e = np.frexp(f64(x))
    hi = np.ldexp(np.trunc(16.0 * m) / 16.0, e)
    return hi, f64(x) - hi


def sigm(f):
    return 1.0 / (1.0 + np.exp(-np.maximum(f, -700.0)))


K, M, N, T, J = 512, 512, 512, 2048, 1024


def setup_inputs():
    n = np.random.standard_normal
    s = mx_kscale(K)[:, None]
    s2 = mx_kscale(M)[:, None]
    h = np.tanh(n((N, T)))
    p_tab = pack_weight(h * s2, "e4m3")
    return {
        "x": (n((K, J)) * s).astype(np.float32),
        "tab_words": p_tab[0],
        "tab_scales": p_tab[1],
        "wz": (n((K, N)) / np.sqrt(K) / s).astype(np.float32),
        "uz": (n((M, N)) / np.sqrt(M) / s2).astype(np.float32),
        "wn": (n((K, N)) / np.sqrt(K) / s).astype(np.float32),
        "un": (n((M, N)) / np.sqrt(M) / s2).astype(np.float32),
        "bz": (0.3 * n(N)).astype(np.float32),
        "bn": (0.3 * n(N)).astype(np.float32),
        "hT": (h).astype(np.float32),
        "wgo": np.tile(np.random.uniform(0.5, 2.0, J), (128, 1)).astype(np.float32),
        "offs": striped(np.random.permutation(T)[:J]),
    }


def reference(x, tab_words, tab_scales, wz, uz, wn, un, bz, bn, hT, wgo, offs):
    idx = unstriped(offs)
    x_ = mxq(f64(x), 0, "e4m3")
    tab_ = unpack_weight(tab_words, tab_scales, "e4m3")[:, idx]
    wz_ = mxq(f64(wz), 0, "e4m3")
    uz_hi, uz_lo = split(uz)
    uz_hi_, uz_lo_ = mxq(uz_hi, 0, "e4m3"), mxq(uz_lo, 0, "e4m3")
    wn_ = mxq(f64(wn), 0, "e4m3")
    un_hi, un_lo = split(un)
    un_hi_, un_lo_ = mxq(un_hi, 0, "e4m3"), mxq(un_lo, 0, "e4m3")
    sz = wz_.T @ x_ + uz_hi_.T @ tab_ + uz_lo_.T @ tab_
    z = sigm(sz + f64(bz)[:, None])
    sn = wn_.T @ x_ + un_hi_.T @ tab_ + un_lo_.T @ tab_
    cd = np.tanh(sn + f64(bn)[:, None])
    out = np.zeros((N, T))
    out[:, idx] = f64(wgo)[0] * (f64(hT)[:, idx] + z * (cd - f64(hT)[:, idx]))
    return out

@@ -1,0 +1,232 @@
+from contextlib import ExitStack
+
+import concourse.mybir as mybir
+from concourse.masks import make_identity
+
+K, M, N, T, J = 512, 512, 512, 2048, 1024
+FLOPS = 2 * 6 * 512 * 512 * 1024
+
+F32 = mybir.dt.float32
+BF16 = mybir.dt.bfloat16
+I32 = mybir.dt.int32
+U32 = mybir.dt.uint32
+U16 = mybir.dt.uint16
+U8 = mybir.dt.uint8
+FP8X4 = mybir.dt.float8_e4m3fn_x4
+ALU = mybir.AluOpType
+ACT = mybir.ActivationFunctionType
+
+P = 128
+PACK = 4
+HALF = 512
+QUART = 256
+NT = N // P
+HI_MASK = -0x000F0010
+
+ADD_PE = True
+MUL_GP = False
+LO_GP = False
+FORCE = True
+
+
+def interleave(nc, dst, src):
+    nc.scalar.copy(dst.rearrange("p (c i) t -> p c t i", i=4), src.rearrange("p t (c i) -> p c t i", i=4))
+
+
+def tile_list_tgn_hl_ema_kernel(
+    tc, x, tab_words, tab_scales, wz, uz, wn, un, bz, bn, hT, wgo, offs, out
+):
+    nc = tc.nc
+    with ExitStack() as ctx:
+        keep = ctx.enter_context(tc.tile_pool(name="keep", bufs=1))
+        ring2 = ctx.enter_context(tc.tile_pool(name="ring2", bufs=2))
+        ring3 = ctx.enter_context(tc.tile_pool(name="ring3", bufs=3))
+        psum = ctx.enter_context(tc.psum_pool(name="psum", bufs=2))
+
+        offsets = keep.tile([P, J // 16], U16, name="offsets")
+        nc.sync.dma_start(offsets[:], offs)
+
+        tabs = keep.tile([P, T], U8, name="tabs", align_bytes=64)
+        nc.gpsimd.memset(tabs[:].bitcast(I32), 0)
+
+        rows = keep.tile([P, P], F32, name="rows")
+        nc.gpsimd.memset(rows[:], 0.0)
+        nc.gpsimd.dma_start(rows[0:NT, :], bz.rearrange("(c p) -> c p", p=P))
+        nc.gpsimd.dma_start(rows[NT : 2 * NT, :], bn.rearrange("(c p) -> c p", p=P))
+        nc.gpsimd.dma_start(rows[2 * NT : 2 * NT + J // P, :], wgo[0, :].rearrange("(b p) -> b p", p=P))
+        ident = keep.tile([P, P], F32, name="ident")
+        make_identity(nc, ident[:])
+        cols_ps = psum.tile([P, HALF], F32, name="t2")
+        nc.tensor.transpose(cols_ps[:, 0:P], rows[:], ident[:])
+        cols_sb = keep.tile([P, 16], F32, name="cols_sb")
+        nc.scalar.copy(cols_sb[:], cols_ps[:, 0:16])
+        neg = keep.tile([P, 2 * NT], F32, name="neg")
+        nc.gpsimd.tensor_scalar(neg[:], cols_sb[:, 0 : 2 * NT], -1.0, 0.0, ALU.mult, ALU.add)
+        bias = cols_sb[:, 0:NT]
+        bias_n = cols_sb[:, NT : 2 * NT]
+        wcol = cols_sb[:, 2 * NT : 16]
+        neg_bz = neg[:, 0:NT]
+        neg_bn = neg[:, NT : 2 * NT]
+
+        pages = [keep.tile([P, T], F32, name="page%d" % i) for i in range(2)]
+        for page in pages:
+            nc.vector.memset(page[:], 0.0)
+
+        raw = {}
+
+        def load_w(name, w, c):
+            t = keep.tile([P, PACK, P], F32, name="raw_%s%d" % (name, c))
+            nc.sync.dma_start(t[:], w[:, c * P : (c + 1) * P].rearrange("(p t) n -> p t n", t=PACK))
+            raw[name, c] = t
+
+        def load_x(q):
+            t = keep.tile([P, PACK, QUART], F32, name="raw_x%d" % q)
+            nc.sync.dma_start(t[:], x[:, q * QUART : (q + 1) * QUART].rearrange("(p t) j -> p t j", t=PACK))
+            raw["x", q] = t
+
+        def load_h(c):
+            t = keep.tile([P, T], F32, name="state%d" % c)
+            nc.sync.dma_start(t[:], hT[c * P : (c + 1) * P, :])
+            raw["h", c] = t
+
+        tabw = keep.tile([P, T], U32, name="tabw", align_bytes=64)
+        load_w("uz", uz, 0)
+        for q in range(4):
+            nc.sync.dma_start(tabs[32 * q : 32 * q + 4, :].bitcast(I32), tab_scales[0, 4 * q : 4 * q + 4, :].bitcast(I32))
+        load_w("un", un, 0)
+        load_x(0)
+        load_x(1)
+        nc.sync.dma_start(tabw[:].bitcast(I32), tab_words[0].rearrange("p t i -> p (t i)").bitcast(I32))
+        load_w("wz", wz, 0)
+        load_w("wn", wn, 0)
+        load_h(0)
+        load_x(2)
+        load_x(3)
+        if not ADD_PE:
+            wrow = keep.tile([P, J], F32, name="wrow")
+            nc.sync.dma_start(wrow[:], wgo)
+        for c in range(1, NT):
+            for name, w in (("uz", uz), ("un", un), ("wz", wz), ("wn", wn)):
+                load_w(name, w, c)
+            load_h(c)
+
+        def lst(h):
+            return offsets[:, h * HALF // 16 : (h + 1) * HALF // 16]
+
+        gw = [keep.tile([P, HALF], U32, name="gw%d" % h, align_bytes=64) for h in range(2)]
+        gs = [keep.tile([P, HALF], U8, name="gs%d" % h, align_bytes=64) for h in range(2)]
+        xq = [keep.tile([P, HALF], U32, name="xq%d" % h, align_bytes=64) for h in range(2)]
+        xs = [keep.tile([P, HALF], U8, name="xs%d" % h, align_bytes=64) for h in range(2)]
+        wq = [keep.tile([P, 6 * P], U32, name="wq%d" % c, align_bytes=64) for c in range(NT)]
+        ws = [keep.tile([P, 6 * P], U8, name="ws%d" % c, align_bytes=64) for c in range(NT)]
+
+        def gather_scales(h):
+            nc.vector.tensor_copy(gs[h][:], tabs[:].indirect(lst(h)))
+
+        def gather_words(h):
+            nc.vector.tensor_copy(gw[h][:], tabw[:].indirect(lst(h)))
+
+        def prep_x(h):
+            xb = ring2.tile([P, HALF, PACK], BF16, name="xb", align_bytes=64)
+            for q in range(2):
+                interleave(nc, xb[:, q * QUART : (q + 1) * QUART, :], raw["x", 2 * h + q][:])
+            nc.vector.quantize_mx(xq[h][:].bitcast(FP8X4), xs[h][:], xb[:].rearrange("p j t -> p (j t)"))
+
+        W = P * PACK
+
+        def prep_u(c):
+            ui = ring2.tile([P, 2 * W], F32, name="ui")
+            ub = ring2.tile([P, 4 * W], BF16, name="ub", align_bytes=64)
+            for g, name in enumerate(("uz", "un")):
+                interleave(nc, ui[:, g * W : (g + 1) * W].rearrange("p (n t) -> p n t", t=PACK), raw[name, c][:])
+            nc.scalar.copy(ub[:, 0 : 2 * W], ui[:].bitcast(BF16)[:, 1::2])
+            hi_words = ub[:, 0 : 2 * W].bitcast(I32)
+            nc.vector.tensor_scalar(hi_words, hi_words, HI_MASK, None, ALU.bitwise_and)
+            eng = nc.gpsimd if LO_GP else nc.vector
+            eng.tensor_tensor(ub[:, 2 * W : 4 * W], ui[:], ub[:, 0 : 2 * W], ALU.subtract)
+            nc.vector.quantize_mx(wq[c][:, 2 * P : 6 * P].bitcast(FP8X4), ws[c][:, 2 * P : 6 * P], ub[:])
+
+        def prep_w(c):
+            wb = ring2.tile([P, 2 * W], BF16, name="wb", align_bytes=64)
+            for g, name in enumerate(("wz", "wn")):
+                interleave(nc, wb[:, g * W : (g + 1) * W].rearrange("p (n t) -> p n t", t=PACK), raw[name, c][:])
+            nc.vector.quantize_mx(wq[c][:, 0 : 2 * P].bitcast(FP8X4), ws[c][:, 0 : 2 * P], wb[:])
+
+        def gate_sum(c, h, g):
+            acc = psum.tile([P, HALF], F32, name="acc%d" % g)
+            for k, (slot, codes, scales) in enumerate(((2 + g, gw[h], gs[h]), (4 + g, gw[h], gs[h]), (g, xq[h], xs[h]))):
+                cols = slice(slot * P, (slot + 1) * P)
+                nc.tensor.matmul_mx(
+                    acc[:], lhsT=wq[c][:, cols].bitcast(FP8X4), lhsT_scale=ws[c][:, cols],
+                    rhs=codes[:].bitcast(FP8X4), rhs_scale=scales[:], start=(k == 0), stop=(k == 2),
+                )
+            return acc
+
+        parts = {}
+
+        def front(u):
+            c, h = divmod(u, 2)
+            acc_z = gate_sum(c, h, 0)
+            acc_n = gate_sum(c, h, 1)
+            zc = ring3.tile([P, HALF], F32, name="zc")
+            nc.scalar.activation(zc[:], acc_z[:], ACT.Sigmoid, bias=neg_bz[:, c : c + 1], scale=-1.0)
+            cn = ring3.tile([P, HALF], F32, name="cn")
+            p1 = ring3.tile([P, HALF], F32, name="p1")
+            p2 = ring3.tile([P, HALF], F32, name="p2")
+            if MUL_GP:
+                z = ring3.tile([P, HALF], F32, name="z")
+                nc.scalar.activation(z[:], acc_z[:], ACT.Sigmoid, bias=bias[:, c : c + 1])
+                nc.scalar.activation(cn[:], acc_n[:], ACT.Tanh, bias=bias_n[:, c : c + 1])
+                nc.gpsimd.tensor_tensor(p2[:], z[:], cn[:], ALU.mult)
+            else:
+                nc.scalar.activation(cn[:], acc_n[:], ACT.Tanh, bias=neg_bn[:, c : c + 1], scale=-1.0)
+                nc.vector.scalar_tensor_tensor(p2[:], zc[:], 1.0, cn[:], ALU.subtract, ALU.mult)
+            nc.vector.tensor_tensor(p1[:], raw["h", c][:].indirect(lst(h)), zc[:], ALU.mult)
+            parts[u] = (p1, p2, cn)
+
+        def back(u):
+            c, h = divmod(u, 2)
+            p1, p2, cn = parts[u]
+            page = pages[c % 2]
+            if FORCE and u + 1 in parts:
+                res = parts[u + 1][2]
+            else:
+                res = ring3.tile([P, HALF], F32, name="res")
+            if ADD_PE:
+                t1 = psum.tile([P, HALF], F32, name="t1")
+                for b in range(4):
+                    cols = slice(b * P, (b + 1) * P)
+                    nc.tensor.matmul(t1[:, cols], p2[:, cols], ident[:], start=True, stop=False, is_transpose=True)
+                    nc.tensor.matmul(t1[:, cols], p1[:, cols], ident[:], start=False, stop=True, is_transpose=True)
+                ut = ring2.tile([P, HALF], F32, name="ut")
+                for b in range(4):
+                    cols = slice(b * P, (b + 1) * P)
+                    nc.scalar.activation(ut[:, cols], t1[:, cols], ACT.Copy, scale=wcol[:, 4 * h + b : 4 * h + b + 1])
+                t2 = psum.tile([P, HALF], F32, name="t2")
+                for b in range(4):
+                    cols = slice(b * P, (b + 1) * P)
+                    nc.tensor.transpose(t2[:, cols], ut[:, cols], ident[:])
+                nc.scalar.copy(res[:], t2[:])
+                nc.vector.tensor_copy(page[:].indirect(lst(h)), res[:])
+            else:
+                nc.vector.tensor_tensor(res[:], p1[:], p2[:], ALU.add)
+                nc.vector.tensor_tensor(page[:].indirect(lst(h)), res[:], wrow[:, h * HALF : (h + 1) * HALF], ALU.mult)
+            if h == 1:
+                nc.sync.dma_start(out[c * P : (c + 1) * P, :], page[:])
+
+        gather_scales(0)
+        gather_scales(1)
+        prep_u(0)
+        prep_x(0)
+        gather_words(0)
+        prep_w(0)
+        front(0)
+        gather_words(1)
+        prep_x(1)
+        for u in range(1, 2 * NT):
+            if u % 2 == 1 and u // 2 + 1 < NT:
+                prep_u(u // 2 + 1)
+                prep_w(u // 2 + 1)
+            front(u)
+            back(u - 1)
+        back(2 * NT - 1)

@@ -4,7 +4,7 @@ import concourse.mybir as mybir
 from concourse.masks import make_identity
 
 K, M, N, T, J = 512, 512, 512, 2048, 1024
-FLOPS = 2 * 6 * 512 * 512 * 1024
+FLOPS = 2 * N * J * (2 * K + 4 * M)
 
 F32 = mybir.dt.float32
 BF16 = mybir.dt.bfloat16
@@ -18,19 +18,24 @@ ACT = mybir.ActivationFunctionType
 
 P = 128
 PACK = 4
-HALF = 512
-QUART = 256
-NT = N // P
+HALF = J // 2
+TILES = N // P
+UNITS = 2 * TILES
+WIDE = P * PACK
+BLOCKS = HALF // P
+Z, CD = 0, 1
+HI, LO, MSG = 0, 1, 2
 HI_MASK = -0x000F0010
-
-ADD_PE = True
-MUL_GP = False
-LO_GP = False
-FORCE = True
+X_ON_VECTOR = (HALF // 2, HALF)
+OWN_GATE_TILES = 3
 
 
-def interleave(nc, dst, src):
-    nc.scalar.copy(dst.rearrange("p (c i) t -> p c t i", i=4), src.rearrange("p t (c i) -> p c t i", i=4))
+def interleave(copy, dst, src):
+    copy(dst.rearrange("p (c i) t -> p c t i", i=4), src.rearrange("p t (c i) -> p c t i", i=4))
+
+
+def by_word(ap):
+    return ap.rearrange("p (w t) -> p w t", t=PACK)
 
 
 def tile_list_tgn_hl_ema_kernel(
@@ -39,194 +44,219 @@ def tile_list_tgn_hl_ema_kernel(
     nc = tc.nc
     with ExitStack() as ctx:
         keep = ctx.enter_context(tc.tile_pool(name="keep", bufs=1))
-        ring2 = ctx.enter_context(tc.tile_pool(name="ring2", bufs=2))
-        ring3 = ctx.enter_context(tc.tile_pool(name="ring3", bufs=3))
-        psum = ctx.enter_context(tc.psum_pool(name="psum", bufs=2))
+        ring = ctx.enter_context(tc.tile_pool(name="ring", bufs=3))
+        psum = ctx.enter_context(tc.psum_pool(name="psum", bufs=1))
 
         offsets = keep.tile([P, J // 16], U16, name="offsets")
         nc.sync.dma_start(offsets[:], offs)
 
-        tabs = keep.tile([P, T], U8, name="tabs", align_bytes=64)
-        nc.gpsimd.memset(tabs[:].bitcast(I32), 0)
+        def entries(half):
+            return offsets[:, half * HALF // 16 : (half + 1) * HALF // 16]
 
         rows = keep.tile([P, P], F32, name="rows")
         nc.gpsimd.memset(rows[:], 0.0)
-        nc.gpsimd.dma_start(rows[0:NT, :], bz.rearrange("(c p) -> c p", p=P))
-        nc.gpsimd.dma_start(rows[NT : 2 * NT, :], bn.rearrange("(c p) -> c p", p=P))
-        nc.gpsimd.dma_start(rows[2 * NT : 2 * NT + J // P, :], wgo[0, :].rearrange("(b p) -> b p", p=P))
+        table_scales = keep.tile([P, T], U8, name="table_scales", align_bytes=64)
+        nc.gpsimd.memset(table_scales[:].bitcast(I32), 0)
         ident = keep.tile([P, P], F32, name="ident")
         make_identity(nc, ident[:])
-        cols_ps = psum.tile([P, HALF], F32, name="t2")
-        nc.tensor.transpose(cols_ps[:, 0:P], rows[:], ident[:])
-        cols_sb = keep.tile([P, 16], F32, name="cols_sb")
-        nc.scalar.copy(cols_sb[:], cols_ps[:, 0:16])
-        neg = keep.tile([P, 2 * NT], F32, name="neg")
-        nc.gpsimd.tensor_scalar(neg[:], cols_sb[:, 0 : 2 * NT], -1.0, 0.0, ALU.mult, ALU.add)
-        bias = cols_sb[:, 0:NT]
-        bias_n = cols_sb[:, NT : 2 * NT]
-        wcol = cols_sb[:, 2 * NT : 16]
-        neg_bz = neg[:, 0:NT]
-        neg_bn = neg[:, NT : 2 * NT]
 
         pages = [keep.tile([P, T], F32, name="page%d" % i) for i in range(2)]
         for page in pages:
             nc.vector.memset(page[:], 0.0)
 
-        raw = {}
+        raw_u, raw_w, raw_x, state = {}, {}, {}, {}
 
-        def load_w(name, w, c):
-            t = keep.tile([P, PACK, P], F32, name="raw_%s%d" % (name, c))
-            nc.sync.dma_start(t[:], w[:, c * P : (c + 1) * P].rearrange("(p t) n -> p t n", t=PACK))
-            raw[name, c] = t
+        def load_weights(into, name, pair, c):
+            for g, w in enumerate(pair):
+                into[c, g] = keep.tile([P, PACK, P], F32, name="%s%d" % (name, 2 * c + g), align_bytes=64)
+                nc.sync.dma_start(into[c, g][:], w[:, c * P : (c + 1) * P].rearrange("(p t) n -> p t n", t=PACK))
 
-        def load_x(q):
-            t = keep.tile([P, PACK, QUART], F32, name="raw_x%d" % q)
-            nc.sync.dma_start(t[:], x[:, q * QUART : (q + 1) * QUART].rearrange("(p t) j -> p t j", t=PACK))
-            raw["x", q] = t
+        def load_u(c):
+            load_weights(raw_u, "raw_u", (uz, un), c)
 
-        def load_h(c):
-            t = keep.tile([P, T], F32, name="state%d" % c)
-            nc.sync.dma_start(t[:], hT[c * P : (c + 1) * P, :])
-            raw["h", c] = t
+        def load_w(c):
+            load_weights(raw_w, "raw_w", (wz, wn), c)
 
-        tabw = keep.tile([P, T], U32, name="tabw", align_bytes=64)
-        load_w("uz", uz, 0)
+        def load_x(half):
+            raw_x[half] = keep.tile([P, PACK, HALF], F32, name="raw_x%d" % half, align_bytes=64)
+            nc.sync.dma_start(raw_x[half][:], x[:, half * HALF : (half + 1) * HALF].rearrange("(p t) j -> p t j", t=PACK))
+
+        def load_state(c):
+            state[c] = keep.tile([P, T], F32, name="state%d" % c)
+            nc.sync.dma_start(state[c][:], hT[c * P : (c + 1) * P, :])
+
+        table_words = keep.tile([P, T], U32, name="table_words", align_bytes=64)
+        load_u(0)
+        nc.sync.dma_start(table_words[:].bitcast(I32), tab_words[0].rearrange("p t i -> p (t i)").bitcast(I32))
+        nc.sync.dma_start(rows[0:TILES, :], bz.rearrange("(c p) -> c p", p=P))
+        nc.sync.dma_start(rows[TILES : 2 * TILES, :], bn.rearrange("(c p) -> c p", p=P))
+        nc.sync.dma_start(rows[2 * TILES : 2 * TILES + J // P, :], wgo[0, :].rearrange("(b p) -> b p", p=P))
+        load_u(1)
         for q in range(4):
-            nc.sync.dma_start(tabs[32 * q : 32 * q + 4, :].bitcast(I32), tab_scales[0, 4 * q : 4 * q + 4, :].bitcast(I32))
-        load_w("un", un, 0)
+            nc.sync.dma_start(
+                table_scales[32 * q : 32 * q + 4, :].bitcast(I32), tab_scales[0, 4 * q : 4 * q + 4, :].bitcast(I32)
+            )
+        load_w(0)
         load_x(0)
+        load_state(0)
+        load_u(2)
         load_x(1)
-        nc.sync.dma_start(tabw[:].bitcast(I32), tab_words[0].rearrange("p t i -> p (t i)").bitcast(I32))
-        load_w("wz", wz, 0)
-        load_w("wn", wn, 0)
-        load_h(0)
-        load_x(2)
-        load_x(3)
-        if not ADD_PE:
-            wrow = keep.tile([P, J], F32, name="wrow")
-            nc.sync.dma_start(wrow[:], wgo)
-        for c in range(1, NT):
-            for name, w in (("uz", uz), ("un", un), ("wz", wz), ("wn", wn)):
-                load_w(name, w, c)
-            load_h(c)
+        load_w(1)
+        load_state(1)
+        load_u(3)
+        for c in range(2, TILES):
+            load_w(c)
+            load_state(c)
 
-        def lst(h):
-            return offsets[:, h * HALF // 16 : (h + 1) * HALF // 16]
+        picked_words = [keep.tile([P, HALF], U32, name="picked_words%d" % h, align_bytes=64) for h in range(2)]
+        picked_scales = {}
+        x_codes = [keep.tile([P, HALF], U32, name="x_codes%d" % h, align_bytes=64) for h in range(2)]
+        x_scales = [keep.tile([P, HALF], U8, name="x_scales%d" % h, align_bytes=64) for h in range(2)]
+        stationary = {}
 
-        gw = [keep.tile([P, HALF], U32, name="gw%d" % h, align_bytes=64) for h in range(2)]
-        gs = [keep.tile([P, HALF], U8, name="gs%d" % h, align_bytes=64) for h in range(2)]
-        xq = [keep.tile([P, HALF], U32, name="xq%d" % h, align_bytes=64) for h in range(2)]
-        xs = [keep.tile([P, HALF], U8, name="xs%d" % h, align_bytes=64) for h in range(2)]
-        wq = [keep.tile([P, 6 * P], U32, name="wq%d" % c, align_bytes=64) for c in range(NT)]
-        ws = [keep.tile([P, 6 * P], U8, name="ws%d" % c, align_bytes=64) for c in range(NT)]
+        def gather_words(half):
+            nc.vector.tensor_copy(picked_words[half][:], table_words[:].indirect(entries(half)))
 
-        def gather_scales(h):
-            nc.vector.tensor_copy(gs[h][:], tabs[:].indirect(lst(h)))
+        def gather_scales(half, after):
+            picked_scales[half] = keep.tile([P, HALF], U8, name="picked_scales%d" % half, tag=after, align_bytes=64)
+            nc.vector.tensor_copy(picked_scales[half][:], table_scales[:].indirect(entries(half)))
 
-        def gather_words(h):
-            nc.vector.tensor_copy(gw[h][:], tabw[:].indirect(lst(h)))
+        def quantise_x(half, after):
+            x_bf = keep.tile([P, HALF, PACK], BF16, name="x_bf%d" % half, tag=after, align_bytes=64)
+            split = X_ON_VECTOR[half]
+            interleave(nc.vector.tensor_copy, x_bf[:, 0:split, :], raw_x[half][:, :, 0:split])
+            if split < HALF:
+                interleave(nc.scalar.copy, x_bf[:, split:HALF, :], raw_x[half][:, :, split:HALF])
+            nc.vector.quantize_mx(x_codes[half][:].bitcast(FP8X4), x_scales[half][:], x_bf[:].rearrange("p j t -> p (j t)"))
 
-        def prep_x(h):
-            xb = ring2.tile([P, HALF, PACK], BF16, name="xb", align_bytes=64)
-            for q in range(2):
-                interleave(nc, xb[:, q * QUART : (q + 1) * QUART, :], raw["x", 2 * h + q][:])
-            nc.vector.quantize_mx(xq[h][:].bitcast(FP8X4), xs[h][:], xb[:].rearrange("p j t -> p (j t)"))
-
-        W = P * PACK
-
-        def prep_u(c):
-            ui = ring2.tile([P, 2 * W], F32, name="ui")
-            ub = ring2.tile([P, 4 * W], BF16, name="ub", align_bytes=64)
-            for g, name in enumerate(("uz", "un")):
-                interleave(nc, ui[:, g * W : (g + 1) * W].rearrange("p (n t) -> p n t", t=PACK), raw[name, c][:])
-            nc.scalar.copy(ub[:, 0 : 2 * W], ui[:].bitcast(BF16)[:, 1::2])
-            hi_words = ub[:, 0 : 2 * W].bitcast(I32)
+        def split_and_quantise(name, c, gates, u32, parts):
+            width = len(gates) * WIDE
+            hi_words = parts[:, 0:width].bitcast(I32)
             nc.vector.tensor_scalar(hi_words, hi_words, HI_MASK, None, ALU.bitwise_and)
-            eng = nc.gpsimd if LO_GP else nc.vector
-            eng.tensor_tensor(ub[:, 2 * W : 4 * W], ui[:], ub[:, 0 : 2 * W], ALU.subtract)
-            nc.vector.quantize_mx(wq[c][:, 2 * P : 6 * P].bitcast(FP8X4), ws[c][:, 2 * P : 6 * P], ub[:])
+            nc.vector.tensor_tensor(parts[:, width : 2 * width], u32[:], parts[:, 0:width], ALU.subtract)
+            codes = keep.tile([P, 2 * len(gates) * P], U32, name="u_codes" + name, align_bytes=64)
+            scales = keep.tile([P, 2 * len(gates) * P], U8, name="u_scales" + name, align_bytes=64)
+            nc.vector.quantize_mx(codes[:].bitcast(FP8X4), scales[:], parts[:])
+            for i, g in enumerate(gates):
+                for part in (HI, LO):
+                    first = (part * len(gates) + i) * P
+                    stationary[c, g, part] = (codes[:, first : first + P], scales[:, first : first + P])
 
-        def prep_w(c):
-            wb = ring2.tile([P, 2 * W], BF16, name="wb", align_bytes=64)
-            for g, name in enumerate(("wz", "wn")):
-                interleave(nc, wb[:, g * W : (g + 1) * W].rearrange("p (n t) -> p n t", t=PACK), raw[name, c][:])
-            nc.vector.quantize_mx(wq[c][:, 0 : 2 * P].bitcast(FP8X4), ws[c][:, 0 : 2 * P], wb[:])
+        def quantise_first_u(g):
+            u32 = keep.tile([P, WIDE], F32, name="u32_first%d" % g, align_bytes=64)
+            parts = keep.tile([P, 2 * WIDE], BF16, name="parts_first%d" % g, align_bytes=64)
+            interleave(nc.vector.tensor_copy, by_word(u32[:]), raw_u[0, g][:])
+            interleave(nc.scalar.copy, by_word(parts[:, 0:WIDE]), raw_u[0, g][:].bitcast(BF16)[:, :, 1::2])
+            split_and_quantise("_first%d" % g, 0, [g], u32, parts)
 
-        def gate_sum(c, h, g):
-            acc = psum.tile([P, HALF], F32, name="acc%d" % g)
-            for k, (slot, codes, scales) in enumerate(((2 + g, gw[h], gs[h]), (4 + g, gw[h], gs[h]), (g, xq[h], xs[h]))):
-                cols = slice(slot * P, (slot + 1) * P)
+        def quantise_u(c, after):
+            u32 = keep.tile([P, 2 * WIDE], F32, name="u32_%d" % c, tag=after, align_bytes=64)
+            parts = keep.tile([P, 4 * WIDE], BF16, name="parts%d" % c, tag="parts%d" % (c % 2), align_bytes=64)
+            for g in (Z, CD):
+                interleave(nc.scalar.copy, by_word(u32[:, g * WIDE : (g + 1) * WIDE]), raw_u[c, g][:])
+            nc.scalar.copy(parts[:, 0 : 2 * WIDE], u32[:].bitcast(BF16)[:, 1::2])
+            split_and_quantise("%d" % c, c, [Z, CD], u32, parts)
+
+        def quantise_w(c, after):
+            w_bf = keep.tile([P, 2 * WIDE], BF16, name="w_bf%d" % c, tag=after, align_bytes=64)
+            for g in (Z, CD):
+                interleave(nc.scalar.copy, by_word(w_bf[:, g * WIDE : (g + 1) * WIDE]), raw_w[c, g][:])
+            codes = keep.tile([P, 2 * P], U32, name="w_codes%d" % c, align_bytes=64)
+            scales = keep.tile([P, 2 * P], U8, name="w_scales%d" % c, align_bytes=64)
+            nc.vector.quantize_mx(codes[:].bitcast(FP8X4), scales[:], w_bf[:])
+            for g in (Z, CD):
+                stationary[c, g, MSG] = (codes[:, g * P : (g + 1) * P], scales[:, g * P : (g + 1) * P])
+
+        def gate_sum(acc, c, half, g):
+            table = (picked_words[half], picked_scales[half])
+            for part, (moving, moving_scales) in ((HI, table), (LO, table), (MSG, (x_codes[half], x_scales[half]))):
+                codes, scales = stationary[c, g, part]
                 nc.tensor.matmul_mx(
-                    acc[:], lhsT=wq[c][:, cols].bitcast(FP8X4), lhsT_scale=ws[c][:, cols],
-                    rhs=codes[:].bitcast(FP8X4), rhs_scale=scales[:], start=(k == 0), stop=(k == 2),
+                    acc[:], lhsT=codes.bitcast(FP8X4), lhsT_scale=scales,
+                    rhs=moving[:].bitcast(FP8X4), rhs_scale=moving_scales[:], start=(part == HI), stop=(part == MSG),
                 )
-            return acc
 
-        parts = {}
+        products, turned = {}, {}
 
-        def front(u):
-            c, h = divmod(u, 2)
-            acc_z = gate_sum(c, h, 0)
-            acc_n = gate_sum(c, h, 1)
-            zc = ring3.tile([P, HALF], F32, name="zc")
-            nc.scalar.activation(zc[:], acc_z[:], ACT.Sigmoid, bias=neg_bz[:, c : c + 1], scale=-1.0)
-            cn = ring3.tile([P, HALF], F32, name="cn")
-            p1 = ring3.tile([P, HALF], F32, name="p1")
-            p2 = ring3.tile([P, HALF], F32, name="p2")
-            if MUL_GP:
-                z = ring3.tile([P, HALF], F32, name="z")
-                nc.scalar.activation(z[:], acc_z[:], ACT.Sigmoid, bias=bias[:, c : c + 1])
-                nc.scalar.activation(cn[:], acc_n[:], ACT.Tanh, bias=bias_n[:, c : c + 1])
-                nc.gpsimd.tensor_tensor(p2[:], z[:], cn[:], ALU.mult)
-            else:
-                nc.scalar.activation(cn[:], acc_n[:], ACT.Tanh, bias=neg_bn[:, c : c + 1], scale=-1.0)
-                nc.vector.scalar_tensor_tensor(p2[:], zc[:], 1.0, cn[:], ALU.subtract, ALU.mult)
-            nc.vector.tensor_tensor(p1[:], raw["h", c][:].indirect(lst(h)), zc[:], ALU.mult)
-            parts[u] = (p1, p2, cn)
+        def gate_tile(name, u):
+            if u < OWN_GATE_TILES:
+                return keep.tile([P, HALF], F32, name="%s%d" % (name, u), align_bytes=64)
+            return ring.tile([P, HALF], F32, name=name)
 
-        def back(u):
-            c, h = divmod(u, 2)
-            p1, p2, cn = parts[u]
-            page = pages[c % 2]
-            if FORCE and u + 1 in parts:
-                res = parts[u + 1][2]
-            else:
-                res = ring3.tile([P, HALF], F32, name="res")
-            if ADD_PE:
-                t1 = psum.tile([P, HALF], F32, name="t1")
-                for b in range(4):
-                    cols = slice(b * P, (b + 1) * P)
-                    nc.tensor.matmul(t1[:, cols], p2[:, cols], ident[:], start=True, stop=False, is_transpose=True)
-                    nc.tensor.matmul(t1[:, cols], p1[:, cols], ident[:], start=False, stop=True, is_transpose=True)
-                ut = ring2.tile([P, HALF], F32, name="ut")
-                for b in range(4):
-                    cols = slice(b * P, (b + 1) * P)
-                    nc.scalar.activation(ut[:, cols], t1[:, cols], ACT.Copy, scale=wcol[:, 4 * h + b : 4 * h + b + 1])
-                t2 = psum.tile([P, HALF], F32, name="t2")
-                for b in range(4):
-                    cols = slice(b * P, (b + 1) * P)
-                    nc.tensor.transpose(t2[:, cols], ut[:, cols], ident[:])
-                nc.scalar.copy(res[:], t2[:])
-                nc.vector.tensor_copy(page[:].indirect(lst(h)), res[:])
-            else:
-                nc.vector.tensor_tensor(res[:], p1[:], p2[:], ALU.add)
-                nc.vector.tensor_tensor(page[:].indirect(lst(h)), res[:], wrow[:, h * HALF : (h + 1) * HALF], ALU.mult)
-            if h == 1:
-                nc.sync.dma_start(out[c * P : (c + 1) * P, :], page[:])
+        def gates_and_products(u):
+            c, half = divmod(u, 2)
+            acc_z = psum.tile([P, HALF], F32, name="acc_z%d" % u, tag="z%d" % half)
+            gate_sum(acc_z, c, half, Z)
+            keep_share = gate_tile("keep_share", u)
+            nc.scalar.activation(keep_share[:], acc_z[:], ACT.Sigmoid, bias=neg_bias[:, c : c + 1], scale=-1.0)
+            acc_cd = psum.tile([P, HALF], F32, name="acc_cd%d" % u, tag="order" if c > 0 else "start")
+            gate_sum(acc_cd, c, half, CD)
+            neg_cd = gate_tile("neg_cd", u)
+            nc.scalar.activation(neg_cd[:], acc_cd[:], ACT.Tanh, bias=neg_bias[:, TILES + c : TILES + c + 1], scale=-1.0)
+            kept = keep.tile([P, HALF], F32, name="kept%d" % u, tag="raw_u%d" % u, align_bytes=64)
+            nc.vector.tensor_tensor(kept[:], state[c][:].indirect(entries(half)), keep_share[:], ALU.mult)
+            fresh = keep.tile([P, HALF], F32, name="fresh%d" % u, tag=("raw_w%d" if c > 0 else "fresh%d") % u, align_bytes=64)
+            nc.vector.scalar_tensor_tensor(fresh[:], keep_share[:], 1.0, neg_cd[:], ALU.subtract, ALU.mult)
+            products[u] = (kept, fresh)
 
-        gather_scales(0)
-        gather_scales(1)
-        prep_u(0)
-        prep_x(0)
+        def add_and_weigh(u, bank):
+            total = psum.tile([P, HALF], F32, name="total%d" % u, tag=bank)
+            for b in range(BLOCKS):
+                cols = slice(b * P, (b + 1) * P)
+                for i, term in enumerate(products[u]):
+                    nc.tensor.matmul(total[:, cols], term[:, cols], ident[:], start=(i == 0), stop=(i == 1), is_transpose=True)
+            turned[u] = ring.tile([P, HALF], F32, name="turned")
+            for b in range(BLOCKS):
+                cols = slice(b * P, (b + 1) * P)
+                block = BLOCKS * (u % 2) + b
+                nc.scalar.activation(turned[u][:, cols], total[:, cols], ACT.Copy, scale=weight[:, block : block + 1])
+
+        def turn_back_and_scatter(u):
+            c, half = divmod(u, 2)
+            back = psum.tile([P, HALF], F32, name="back%d" % u, tag="order" if u > 0 else "start")
+            for b in range(BLOCKS):
+                cols = slice(b * P, (b + 1) * P)
+                nc.tensor.transpose(back[:, cols], turned[u][:, cols], ident[:])
+            result = ring.tile([P, HALF], F32, name="result")
+            nc.scalar.copy(result[:], back[:])
+            nc.vector.tensor_copy(pages[c % 2][:].indirect(entries(half)), result[:])
+            if half == 1:
+                nc.sync.dma_start(out[c * P : (c + 1) * P, :], pages[c % 2][:])
+
+        for g in (Z, CD):
+            quantise_first_u(g)
         gather_words(0)
-        prep_w(0)
-        front(0)
         gather_words(1)
-        prep_x(1)
-        for u in range(1, 2 * NT):
-            if u % 2 == 1 and u // 2 + 1 < NT:
-                prep_u(u // 2 + 1)
-                prep_w(u // 2 + 1)
-            front(u)
-            back(u - 1)
-        back(2 * NT - 1)
+        gather_scales(0, after="table_words")
+        quantise_u(1, after="u32_1")
+        quantise_w(0, after="w_bf0")
+
+        columns = psum.tile([P, HALF], F32, name="columns")
+        nc.tensor.transpose(columns[:, 0:P], rows[:], ident[:])
+        neg_bias = keep.tile([P, 2 * TILES], F32, name="neg_bias", tag="raw_w0", align_bytes=64)
+        nc.scalar.activation(neg_bias[:], columns[:, 0 : 2 * TILES], ACT.Copy, scale=-1.0)
+        weight = keep.tile([P, J // P], F32, name="weight", tag="raw_w1", align_bytes=64)
+        nc.scalar.copy(weight[:], columns[:, 2 * TILES : 2 * TILES + J // P])
+
+        quantise_x(0, after="x_bf0")
+        gather_scales(1, after="x_bf0")
+        gates_and_products(0)
+        quantise_x(1, after="neg_cd0")
+        add_and_weigh(0, "z0")
+        quantise_u(2, after="keep_share0")
+        gates_and_products(1)
+        quantise_w(1, after="raw_x1")
+        turn_back_and_scatter(0)
+
+        for u in range(2, UNITS):
+            gates_and_products(u)
+            add_and_weigh(u - 1, "z%d" % ((u - 1) % 2))
+            if u == 2:
+                quantise_u(TILES - 1, after="neg_cd1")
+            else:
+                turn_back_and_scatter(u - 2)
+            if u < TILES:
+                quantise_w(u, after="keep_share%d" % (u - 1))
+        turn_back_and_scatter(UNITS - 2)
+        add_and_weigh(UNITS - 1, "order")
+        turn_back_and_scatter(UNITS - 1)

@@ -53,10 +53,10 @@ def tile_list_tgn_hl_ema_kernel(
         def entries(half):
             return offsets[:, half * HALF // 16 : (half + 1) * HALF // 16]
 
-        rows = keep.tile([P, P], F32, name="rows")
-        nc.gpsimd.memset(rows[:], 0.0)
         table_scales = keep.tile([P, T], U8, name="table_scales", align_bytes=64)
         nc.gpsimd.memset(table_scales[:].bitcast(I32), 0)
+        rows = keep.tile([P, P], F32, name="rows")
+        nc.gpsimd.memset(rows[:], 0.0)
         ident = keep.tile([P, P], F32, name="ident")
         make_identity(nc, ident[:])
 
@@ -88,16 +88,16 @@ def tile_list_tgn_hl_ema_kernel(
         table_words = keep.tile([P, T], U32, name="table_words", align_bytes=64)
         load_u(0)
         nc.sync.dma_start(table_words[:].bitcast(I32), tab_words[0].rearrange("p t i -> p (t i)").bitcast(I32))
-        nc.sync.dma_start(rows[0:TILES, :], bz.rearrange("(c p) -> c p", p=P))
-        nc.sync.dma_start(rows[TILES : 2 * TILES, :], bn.rearrange("(c p) -> c p", p=P))
-        nc.sync.dma_start(rows[2 * TILES : 2 * TILES + J // P, :], wgo[0, :].rearrange("(b p) -> b p", p=P))
-        load_u(1)
         for q in range(4):
             nc.sync.dma_start(
                 table_scales[32 * q : 32 * q + 4, :].bitcast(I32), tab_scales[0, 4 * q : 4 * q + 4, :].bitcast(I32)
             )
+        load_u(1)
         load_w(0)
         load_x(0)
+        nc.sync.dma_start(rows[0:TILES, :], bz.rearrange("(c p) -> c p", p=P))
+        nc.sync.dma_start(rows[TILES : 2 * TILES, :], bn.rearrange("(c p) -> c p", p=P))
+        nc.sync.dma_start(rows[2 * TILES : 2 * TILES + J // P, :], wgo[0, :].rearrange("(b p) -> b p", p=P))
         load_state(0)
         load_u(2)
         load_x(1)
@@ -145,7 +145,7 @@ def tile_list_tgn_hl_ema_kernel(
         def quantise_first_u(g):
             u32 = keep.tile([P, WIDE], F32, name="u32_first%d" % g, align_bytes=64)
             parts = keep.tile([P, 2 * WIDE], BF16, name="parts_first%d" % g, align_bytes=64)
-            interleave(nc.vector.tensor_copy, by_word(u32[:]), raw_u[0, g][:])
+            nc.vector.tensor_copy(by_word(u32[:]), raw_u[0, g][:].rearrange("p t n -> p n t"))
             interleave(nc.scalar.copy, by_word(parts[:, 0:WIDE]), raw_u[0, g][:].bitcast(BF16)[:, :, 1::2])
             split_and_quantise("_first%d" % g, 0, [g], u32, parts)
 
@@ -189,7 +189,7 @@ def tile_list_tgn_hl_ema_kernel(
             gate_sum(acc_z, c, half, Z)
             keep_share = gate_tile("keep_share", u)
             nc.scalar.activation(keep_share[:], acc_z[:], ACT.Sigmoid, bias=neg_bias[:, c : c + 1], scale=-1.0)
-            acc_cd = psum.tile([P, HALF], F32, name="acc_cd%d" % u, tag="order" if c > 0 else "start")
+            acc_cd = psum.tile([P, HALF], F32, name="acc_cd%d" % u, tag="order%d" % half if c > 0 else "start")
             gate_sum(acc_cd, c, half, CD)
             neg_cd = gate_tile("neg_cd", u)
             nc.scalar.activation(neg_cd[:], acc_cd[:], ACT.Tanh, bias=neg_bias[:, TILES + c : TILES + c + 1], scale=-1.0)
@@ -213,7 +213,7 @@ def tile_list_tgn_hl_ema_kernel(
 
         def turn_back_and_scatter(u):
             c, half = divmod(u, 2)
-            back = psum.tile([P, HALF], F32, name="back%d" % u, tag="order" if u > 0 else "start")
+            back = psum.tile([P, HALF], F32, name="back%d" % u, tag="order%d" % half if u > 0 else "start")
             for b in range(BLOCKS):
                 cols = slice(b * P, (b + 1) * P)
                 nc.tensor.transpose(back[:, cols], turned[u][:, cols], ident[:])
@@ -221,7 +221,10 @@ def tile_list_tgn_hl_ema_kernel(
             nc.scalar.copy(result[:], back[:])
             nc.vector.tensor_copy(pages[c % 2][:].indirect(entries(half)), result[:])
             if half == 1:
-                nc.sync.dma_start(out[c * P : (c + 1) * P, :], pages[c % 2][:])
+                queues = (nc.sync, nc.scalar) if c == TILES - 1 else (nc.sync,)
+                for i, queue in enumerate(queues):
+                    cols = slice(i * T // len(queues), (i + 1) * T // len(queues))
+                    queue.dma_start(out[c * P : (c + 1) * P, cols], pages[c % 2][:, cols])
 
         for g in (Z, CD):
             quantise_first_u(g)
@@ -258,5 +261,5 @@ def tile_list_tgn_hl_ema_kernel(
             if u < TILES:
                 quantise_w(u, after="keep_share%d" % (u - 1))
         turn_back_and_scatter(UNITS - 2)
-        add_and_weigh(UNITS - 1, "order")
+        add_and_weigh(UNITS - 1, "order0")
         turn_back_and_scatter(UNITS - 1)

@@ -26,8 +26,8 @@ BLOCKS = HALF // P
 Z, CD = 0, 1
 HI, LO, MSG = 0, 1, 2
 HI_MASK = -0x000F0010
+FIRST_ON_GPSIMD = 3
 X_ON_VECTOR = (HALF // 2, HALF)
-OWN_GATE_TILES = 3
 
 
 def interleave(copy, dst, src):
@@ -178,26 +178,22 @@ def tile_list_tgn_hl_ema_kernel(
 
         products, turned = {}, {}
 
-        def gate_tile(name, u):
-            if u < OWN_GATE_TILES:
-                return keep.tile([P, HALF], F32, name="%s%d" % (name, u), align_bytes=64)
-            return ring.tile([P, HALF], F32, name=name)
-
         def gates_and_products(u):
             c, half = divmod(u, 2)
-            acc_z = psum.tile([P, HALF], F32, name="acc_z%d" % u, tag="z%d" % half)
-            gate_sum(acc_z, c, half, Z)
-            keep_share = gate_tile("keep_share", u)
-            nc.scalar.activation(keep_share[:], acc_z[:], ACT.Sigmoid, bias=neg_bias[:, c : c + 1], scale=-1.0)
             acc_cd = psum.tile([P, HALF], F32, name="acc_cd%d" % u, tag="order%d" % half if c > 0 else "start")
             gate_sum(acc_cd, c, half, CD)
-            neg_cd = gate_tile("neg_cd", u)
-            nc.scalar.activation(neg_cd[:], acc_cd[:], ACT.Tanh, bias=neg_bias[:, TILES + c : TILES + c + 1], scale=-1.0)
-            kept = keep.tile([P, HALF], F32, name="kept%d" % u, tag="raw_u%d" % u, align_bytes=64)
-            nc.vector.tensor_tensor(kept[:], state[c][:].indirect(entries(half)), keep_share[:], ALU.mult)
-            fresh = keep.tile([P, HALF], F32, name="fresh%d" % u, tag=("raw_w%d" if c > 0 else "fresh%d") % u, align_bytes=64)
-            nc.vector.scalar_tensor_tensor(fresh[:], keep_share[:], 1.0, neg_cd[:], ALU.subtract, ALU.mult)
-            products[u] = (kept, fresh)
+            cd = keep.tile([P, HALF], F32, name="cd%d" % u, tag="hand%d" % (u % 3))
+            nc.scalar.activation(cd[:], acc_cd[:], ACT.Tanh, bias=plain[:, c : c + 1])
+            acc_z = psum.tile([P, HALF], F32, name="acc_z%d" % u, tag="z%d" % half)
+            gate_sum(acc_z, c, half, Z)
+            keep_share = keep.tile([P, HALF], F32, name="keep_share%d" % u, align_bytes=64)
+            nc.scalar.activation(keep_share[:], acc_z[:], ACT.Sigmoid, bias=neg_bz[:, c : c + 1], scale=-1.0)
+            gap = keep.tile([P, HALF], F32, name="gap%d" % u, tag="raw_u%d" % u, align_bytes=64)
+            nc.vector.tensor_tensor(gap[:], state[c][:].indirect(entries(half)), cd[:], ALU.subtract)
+            kept = keep.tile([P, HALF], F32, name="kept%d" % u, tag=("raw_w%d" if c > 0 else "kept%d") % u, align_bytes=64)
+            engine = nc.gpsimd if u >= FIRST_ON_GPSIMD else nc.vector
+            engine.tensor_tensor(kept[:], gap[:], keep_share[:], ALU.mult)
+            products[u] = (kept, cd)
 
         def add_and_weigh(u, bank):
             total = psum.tile([P, HALF], F32, name="total%d" % u, tag=bank)
@@ -205,11 +201,11 @@ def tile_list_tgn_hl_ema_kernel(
                 cols = slice(b * P, (b + 1) * P)
                 for i, term in enumerate(products[u]):
                     nc.tensor.matmul(total[:, cols], term[:, cols], ident[:], start=(i == 0), stop=(i == 1), is_transpose=True)
-            turned[u] = ring.tile([P, HALF], F32, name="turned")
+            turned[u] = keep.tile([P, HALF], F32, name="turned%d" % u, tag="hand%d" % (u % 3))
             for b in range(BLOCKS):
                 cols = slice(b * P, (b + 1) * P)
-                block = BLOCKS * (u % 2) + b
-                nc.scalar.activation(turned[u][:, cols], total[:, cols], ACT.Copy, scale=weight[:, block : block + 1])
+                block = TILES + BLOCKS * (u % 2) + b
+                nc.scalar.activation(turned[u][:, cols], total[:, cols], ACT.Copy, scale=plain[:, block : block + 1])
 
         def turn_back_and_scatter(u):
             c, half = divmod(u, 2)
@@ -236,15 +232,15 @@ def tile_list_tgn_hl_ema_kernel(
 
         columns = psum.tile([P, HALF], F32, name="columns")
         nc.tensor.transpose(columns[:, 0:P], rows[:], ident[:])
-        neg_bias = keep.tile([P, 2 * TILES], F32, name="neg_bias", tag="raw_w0", align_bytes=64)
-        nc.scalar.activation(neg_bias[:], columns[:, 0 : 2 * TILES], ACT.Copy, scale=-1.0)
-        weight = keep.tile([P, J // P], F32, name="weight", tag="raw_w1", align_bytes=64)
-        nc.scalar.copy(weight[:], columns[:, 2 * TILES : 2 * TILES + J // P])
+        neg_bz = keep.tile([P, TILES], F32, name="neg_bz", tag="raw_w0", align_bytes=64)
+        nc.scalar.activation(neg_bz[:], columns[:, 0:TILES], ACT.Copy, scale=-1.0)
+        plain = keep.tile([P, TILES + J // P], F32, name="plain", tag="raw_w1", align_bytes=64)
+        nc.scalar.copy(plain[:], columns[:, TILES : 2 * TILES + J // P])
 
         quantise_x(0, after="x_bf0")
         gather_scales(1, after="x_bf0")
         gates_and_products(0)
-        quantise_x(1, after="neg_cd0")
+        quantise_x(1, after="raw_u0")
         add_and_weigh(0, "z0")
         quantise_u(2, after="keep_share0")
         gates_and_products(1)
@@ -253,11 +249,11 @@ def tile_list_tgn_hl_ema_kernel(
 
         for u in range(2, UNITS):
             gates_and_products(u)
-            add_and_weigh(u - 1, "z%d" % ((u - 1) % 2))
-            if u == 2:
-                quantise_u(TILES - 1, after="neg_cd1")
-            else:
+            if u > 2:
                 turn_back_and_scatter(u - 2)
+            add_and_weigh(u - 1, "order%d" % (u % 2) if u > 2 else "start")
+            if u == 2:
+                quantise_u(TILES - 1, after="raw_u1")
             if u < TILES:
                 quantise_w(u, after="keep_share%d" % (u - 1))
         turn_back_and_scatter(UNITS - 2)

from contextlib import ExitStack

import concourse.mybir as mybir
from concourse.masks import make_identity

K, M, N, T, J = 512, 512, 512, 2048, 1024
FLOPS = 2 * N * J * (2 * K + 4 * M)

F32 = mybir.dt.float32
BF16 = mybir.dt.bfloat16
I32 = mybir.dt.int32
U32 = mybir.dt.uint32
U16 = mybir.dt.uint16
U8 = mybir.dt.uint8
FP8X4 = mybir.dt.float8_e4m3fn_x4
ALU = mybir.AluOpType
ACT = mybir.ActivationFunctionType

P = 128
PACK = 4
HALF = J // 2
TILES = N // P
UNITS = 2 * TILES
WIDE = P * PACK
BLOCKS = HALF // P
Z, CD = 0, 1
HI, LO, MSG = 0, 1, 2
HI_MASK = -0x000F0010
FIRST_ON_GPSIMD = 3
X_ON_VECTOR = (HALF // 2, HALF)


def interleave(copy, dst, src):
    copy(dst.rearrange("p (c i) t -> p c t i", i=4), src.rearrange("p t (c i) -> p c t i", i=4))


def by_word(ap):
    return ap.rearrange("p (w t) -> p w t", t=PACK)


def tile_list_tgn_hl_ema_kernel(
    tc, x, tab_words, tab_scales, wz, uz, wn, un, bz, bn, hT, wgo, offs, out
):
    nc = tc.nc
    with ExitStack() as ctx:
        keep = ctx.enter_context(tc.tile_pool(name="keep", bufs=1))
        ring = ctx.enter_context(tc.tile_pool(name="ring", bufs=3))
        psum = ctx.enter_context(tc.psum_pool(name="psum", bufs=1))

        offsets = keep.tile([P, J // 16], U16, name="offsets")
        nc.sync.dma_start(offsets[:], offs)

        def entries(half):
            return offsets[:, half * HALF // 16 : (half + 1) * HALF // 16]

        table_scales = keep.tile([P, T], U8, name="table_scales", align_bytes=64)
        nc.gpsimd.memset(table_scales[:].bitcast(I32), 0)
        rows = keep.tile([P, P], F32, name="rows")
        nc.gpsimd.memset(rows[:], 0.0)
        ident = keep.tile([P, P], F32, name="ident")
        make_identity(nc, ident[:])

        pages = [keep.tile([P, T], F32, name="page%d" % i) for i in range(2)]
        for page in pages:
            nc.vector.memset(page[:], 0.0)

        raw_u, raw_w, raw_x, state = {}, {}, {}, {}

        def load_weights(into, name, pair, c):
            for g, w in enumerate(pair):
                into[c, g] = keep.tile([P, PACK, P], F32, name="%s%d" % (name, 2 * c + g), align_bytes=64)
                nc.sync.dma_start(into[c, g][:], w[:, c * P : (c + 1) * P].rearrange("(p t) n -> p t n", t=PACK))

        def load_u(c):
            load_weights(raw_u, "raw_u", (uz, un), c)

        def load_w(c):
            load_weights(raw_w, "raw_w", (wz, wn), c)

        def load_x(half):
            raw_x[half] = keep.tile([P, PACK, HALF], F32, name="raw_x%d" % half, align_bytes=64)
            nc.sync.dma_start(raw_x[half][:], x[:, half * HALF : (half + 1) * HALF].rearrange("(p t) j -> p t j", t=PACK))

        def load_state(c):
            state[c] = keep.tile([P, T], F32, name="state%d" % c)
            nc.sync.dma_start(state[c][:], hT[c * P : (c + 1) * P, :])

        table_words = keep.tile([P, T], U32, name="table_words", align_bytes=64)
        load_u(0)
        nc.sync.dma_start(table_words[:].bitcast(I32), tab_words[0].rearrange("p t i -> p (t i)").bitcast(I32))
        for q in range(4):
            nc.sync.dma_start(
                table_scales[32 * q : 32 * q + 4, :].bitcast(I32), tab_scales[0, 4 * q : 4 * q + 4, :].bitcast(I32)
            )
        load_u(1)
        load_w(0)
        load_x(0)
        nc.sync.dma_start(rows[0:TILES, :], bz.rearrange("(c p) -> c p", p=P))
        nc.sync.dma_start(rows[TILES : 2 * TILES, :], bn.rearrange("(c p) -> c p", p=P))
        nc.sync.dma_start(rows[2 * TILES : 2 * TILES + J // P, :], wgo[0, :].rearrange("(b p) -> b p", p=P))
        load_state(0)
        load_u(2)
        load_x(1)
        load_w(1)
        load_state(1)
        load_u(3)
        for c in range(2, TILES):
            load_w(c)
            load_state(c)

        picked_words = [keep.tile([P, HALF], U32, name="picked_words%d" % h, align_bytes=64) for h in range(2)]
        picked_scales = {}
        x_codes = [keep.tile([P, HALF], U32, name="x_codes%d" % h, align_bytes=64) for h in range(2)]
        x_scales = [keep.tile([P, HALF], U8, name="x_scales%d" % h, align_bytes=64) for h in range(2)]
        stationary = {}

        def gather_words(half):
            nc.vector.tensor_copy(picked_words[half][:], table_words[:].indirect(entries(half)))

        def gather_scales(half, after):
            picked_scales[half] = keep.tile([P, HALF], U8, name="picked_scales%d" % half, tag=after, align_bytes=64)
            nc.vector.tensor_copy(picked_scales[half][:], table_scales[:].indirect(entries(half)))

        def quantise_x(half, after):
            x_bf = keep.tile([P, HALF, PACK], BF16, name="x_bf%d" % half, tag=after, align_bytes=64)
            split = X_ON_VECTOR[half]
            interleave(nc.vector.tensor_copy, x_bf[:, 0:split, :], raw_x[half][:, :, 0:split])
            if split < HALF:
                interleave(nc.scalar.copy, x_bf[:, split:HALF, :], raw_x[half][:, :, split:HALF])
            nc.vector.quantize_mx(x_codes[half][:].bitcast(FP8X4), x_scales[half][:], x_bf[:].rearrange("p j t -> p (j t)"))

        def split_and_quantise(name, c, gates, u32, parts):
            width = len(gates) * WIDE
            hi_words = parts[:, 0:width].bitcast(I32)
            nc.vector.tensor_scalar(hi_words, hi_words, HI_MASK, None, ALU.bitwise_and)
            nc.vector.tensor_tensor(parts[:, width : 2 * width], u32[:], parts[:, 0:width], ALU.subtract)
            codes = keep.tile([P, 2 * len(gates) * P], U32, name="u_codes" + name, align_bytes=64)
            scales = keep.tile([P, 2 * len(gates) * P], U8, name="u_scales" + name, align_bytes=64)
            nc.vector.quantize_mx(codes[:].bitcast(FP8X4), scales[:], parts[:])
            for i, g in enumerate(gates):
                for part in (HI, LO):
                    first = (part * len(gates) + i) * P
                    stationary[c, g, part] = (codes[:, first : first + P], scales[:, first : first + P])

        def quantise_first_u(g):
            u32 = keep.tile([P, WIDE], F32, name="u32_first%d" % g, align_bytes=64)
            parts = keep.tile([P, 2 * WIDE], BF16, name="parts_first%d" % g, align_bytes=64)
            nc.vector.tensor_copy(by_word(u32[:]), raw_u[0, g][:].rearrange("p t n -> p n t"))
            interleave(nc.scalar.copy, by_word(parts[:, 0:WIDE]), raw_u[0, g][:].bitcast(BF16)[:, :, 1::2])
            split_and_quantise("_first%d" % g, 0, [g], u32, parts)

        def quantise_u(c, after):
            u32 = keep.tile([P, 2 * WIDE], F32, name="u32_%d" % c, tag=after, align_bytes=64)
            parts = keep.tile([P, 4 * WIDE], BF16, name="parts%d" % c, tag="parts%d" % (c % 2), align_bytes=64)
            for g in (Z, CD):
                interleave(nc.scalar.copy, by_word(u32[:, g * WIDE : (g + 1) * WIDE]), raw_u[c, g][:])
            nc.scalar.copy(parts[:, 0 : 2 * WIDE], u32[:].bitcast(BF16)[:, 1::2])
            split_and_quantise("%d" % c, c, [Z, CD], u32, parts)

        def quantise_w(c, after):
            w_bf = keep.tile([P, 2 * WIDE], BF16, name="w_bf%d" % c, tag=after, align_bytes=64)
            for g in (Z, CD):
                interleave(nc.scalar.copy, by_word(w_bf[:, g * WIDE : (g + 1) * WIDE]), raw_w[c, g][:])
            codes = keep.tile([P, 2 * P], U32, name="w_codes%d" % c, align_bytes=64)
            scales = keep.tile([P, 2 * P], U8, name="w_scales%d" % c, align_bytes=64)
            nc.vector.quantize_mx(codes[:].bitcast(FP8X4), scales[:], w_bf[:])
            for g in (Z, CD):
                stationary[c, g, MSG] = (codes[:, g * P : (g + 1) * P], scales[:, g * P : (g + 1) * P])

        def gate_sum(acc, c, half, g):
            table = (picked_words[half], picked_scales[half])
            for part, (moving, moving_scales) in ((HI, table), (LO, table), (MSG, (x_codes[half], x_scales[half]))):
                codes, scales = stationary[c, g, part]
                nc.tensor.matmul_mx(
                    acc[:], lhsT=codes.bitcast(FP8X4), lhsT_scale=scales,
                    rhs=moving[:].bitcast(FP8X4), rhs_scale=moving_scales[:], start=(part == HI), stop=(part == MSG),
                )

        products, turned = {}, {}

        def gates_and_products(u):
            c, half = divmod(u, 2)
            acc_cd = psum.tile([P, HALF], F32, name="acc_cd%d" % u, tag="order%d" % half if c > 0 else "start")
            gate_sum(acc_cd, c, half, CD)
            cd = keep.tile([P, HALF], F32, name="cd%d" % u, tag="hand%d" % (u % 3))
            nc.scalar.activation(cd[:], acc_cd[:], ACT.Tanh, bias=plain[:, c : c + 1])
            acc_z = psum.tile([P, HALF], F32, name="acc_z%d" % u, tag="z%d" % half)
            gate_sum(acc_z, c, half, Z)
            keep_share = keep.tile([P, HALF], F32, name="keep_share%d" % u, align_bytes=64)
            nc.scalar.activation(keep_share[:], acc_z[:], ACT.Sigmoid, bias=neg_bz[:, c : c + 1], scale=-1.0)
            gap = keep.tile([P, HALF], F32, name="gap%d" % u, tag="raw_u%d" % u, align_bytes=64)
            nc.vector.tensor_tensor(gap[:], state[c][:].indirect(entries(half)), cd[:], ALU.subtract)
            kept = keep.tile([P, HALF], F32, name="kept%d" % u, tag=("raw_w%d" if c > 0 else "kept%d") % u, align_bytes=64)
            engine = nc.gpsimd if u >= FIRST_ON_GPSIMD else nc.vector
            engine.tensor_tensor(kept[:], gap[:], keep_share[:], ALU.mult)
            products[u] = (kept, cd)

        def add_and_weigh(u, bank):
            total = psum.tile([P, HALF], F32, name="total%d" % u, tag=bank)
            for b in range(BLOCKS):
                cols = slice(b * P, (b + 1) * P)
                for i, term in enumerate(products[u]):
                    nc.tensor.matmul(total[:, cols], term[:, cols], ident[:], start=(i == 0), stop=(i == 1), is_transpose=True)
            turned[u] = keep.tile([P, HALF], F32, name="turned%d" % u, tag="hand%d" % (u % 3))
            for b in range(BLOCKS):
                cols = slice(b * P, (b + 1) * P)
                block = TILES + BLOCKS * (u % 2) + b
                nc.scalar.activation(turned[u][:, cols], total[:, cols], ACT.Copy, scale=plain[:, block : block + 1])

        def turn_back_and_scatter(u):
            c, half = divmod(u, 2)
            back = psum.tile([P, HALF], F32, name="back%d" % u, tag="order%d" % half if u > 0 else "start")
            for b in range(BLOCKS):
                cols = slice(b * P, (b + 1) * P)
                nc.tensor.transpose(back[:, cols], turned[u][:, cols], ident[:])
            result = ring.tile([P, HALF], F32, name="result")
            nc.scalar.copy(result[:], back[:])
            nc.vector.tensor_copy(pages[c % 2][:].indirect(entries(half)), result[:])
            if half == 1:
                queues = (nc.sync, nc.scalar) if c == TILES - 1 else (nc.sync,)
                for i, queue in enumerate(queues):
                    cols = slice(i * T // len(queues), (i + 1) * T // len(queues))
                    queue.dma_start(out[c * P : (c + 1) * P, cols], pages[c % 2][:, cols])

        for g in (Z, CD):
            quantise_first_u(g)
        gather_words(0)
        gather_words(1)
        gather_scales(0, after="table_words")
        quantise_u(1, after="u32_1")
        quantise_w(0, after="w_bf0")

        columns = psum.tile([P, HALF], F32, name="columns")
        nc.tensor.transpose(columns[:, 0:P], rows[:], ident[:])
        neg_bz = keep.tile([P, TILES], F32, name="neg_bz", tag="raw_w0", align_bytes=64)
        nc.scalar.activation(neg_bz[:], columns[:, 0:TILES], ACT.Copy, scale=-1.0)
        plain = keep.tile([P, TILES + J // P], F32, name="plain", tag="raw_w1", align_bytes=64)
        nc.scalar.copy(plain[:], columns[:, TILES : 2 * TILES + J // P])

        quantise_x(0, after="x_bf0")
        gather_scales(1, after="x_bf0")
        gates_and_products(0)
        quantise_x(1, after="raw_u0")
        add_and_weigh(0, "z0")
        quantise_u(2, after="keep_share0")
        gates_and_products(1)
        quantise_w(1, after="raw_x1")
        turn_back_and_scatter(0)

        for u in range(2, UNITS):
            gates_and_products(u)
            if u > 2:
                turn_back_and_scatter(u - 2)
            add_and_weigh(u - 1, "order%d" % (u % 2) if u > 2 else "start")
            if u == 2:
                quantise_u(TILES - 1, after="raw_u1")
            if u < TILES:
                quantise_w(u, after="keep_share%d" % (u - 1))
        turn_back_and_scatter(UNITS - 2)
        add_and_weigh(UNITS - 1, "order0")
        turn_back_and_scatter(UNITS - 1)
